import numpy as np, ml_dtypes
CORES = [24,25,26,27,48,49,50,51,72,73,74,75,96,97,98,99]
N = 16
C = 256
SIGN = [[1,1,1,1,1,1,1,1,1,1,1,1,1,1,1,1],[1,-1,1,-1,1,-1,1,-1,1,-1,1,-1,1,-1,1,-1],[1,1,-1,-1,1,1,-1,-1,1,1,-1,-1,1,1,-1,-1],[1,-1,-1,1,1,-1,-1,1,1,-1,-1,1,1,-1,-1,1],[1,1,1,1,-1,-1,-1,-1,1,1,1,1,-1,-1,-1,-1],[1,-1,1,-1,-1,1,-1,1,1,-1,1,-1,-1,1,-1,1],[1,1,-1,-1,-1,-1,1,1,1,1,-1,-1,-1,-1,1,1],[1,-1,-1,1,-1,1,1,-1,1,-1,-1,1,-1,1,1,-1],[1,1,1,1,1,1,1,1,-1,-1,-1,-1,-1,-1,-1,-1],[1,-1,1,-1,1,-1,1,-1,-1,1,-1,1,-1,1,-1,1],[1,1,-1,-1,1,1,-1,-1,-1,-1,1,1,-1,-1,1,1],[1,-1,-1,1,1,-1,-1,1,-1,1,1,-1,-1,1,1,-1],[1,1,1,1,-1,-1,-1,-1,-1,-1,-1,-1,1,1,1,1],[1,-1,1,-1,-1,1,-1,1,-1,1,-1,1,1,-1,1,-1],[1,1,-1,-1,-1,-1,1,1,-1,-1,1,1,1,1,-1,-1],[1,-1,-1,1,-1,1,1,-1,-1,1,1,-1,1,-1,-1,1]]
def setup_inputs(rng):
    return {"x": rng.standard_normal((N, 128, C), dtype=np.float32).astype(ml_dtypes.bfloat16)}
def setup_inputs_big(rng):
    d = setup_inputs(rng)
    for k in ("x",): d[k] = (d[k].astype(np.float32) * 1048576.0).astype(d[k].dtype)
    return d
def setup_inputs_small(rng):
    d = setup_inputs(rng)
    for k in ("x",): d[k] = (d[k].astype(np.float32) * (1 / 1048576.0)).astype(d[k].dtype)
    return d
def setup_inputs_apart(rng):
    d = setup_inputs(rng)
    f = (10.0 ** rng.permutation(np.linspace(-1.5, 1.5, N))).astype(np.float32).reshape(N, 1, 1)
    for k in ("x",): d[k] = (d[k].astype(np.float32) * f).astype(d[k].dtype)
    return d
def reference(x):
    X = x.astype(np.float64)
    y = np.stack([sum(SIGN[r][j] * X[j] for j in range(N)) for r in range(N)])
    return {"y": y.astype(ml_dtypes.bfloat16)}

@@ -1,0 +1,205 @@
+from concourse.bass import DstId, RemoteDMATransfer
+from concourse.mybir import AluOpType
+
+NSIM = 112
+P, C = 128, 256
+
+SCRATCH = {
+    "xs": ("sbuf", [P, C], "bfloat16"),
+    "nx": ("sbuf", [P, C], "bfloat16"),
+    "ys": ("sbuf", [P, C], "bfloat16"),
+    "zp": ("psum", [P, C], "float32"),
+    "pa": ("psum", [P, C], "float32"),
+    "pb": ("psum", [P, C], "float32"),
+}
+for _i in range(4):
+    SCRATCH["Lp%d" % _i] = ("sbuf", [P, C], "bfloat16")
+    SCRATCH["Lm%d" % _i] = ("sbuf", [P, C], "bfloat16")
+    SCRATCH["U%d" % _i] = ("sbuf", [P, C], "bfloat16")
+SEMAPHORES = ["ld", "vz", "neg", "xin", "sent", "vc", "fin", "st", "u0", "u1", "u2", "u3"]
+
+
+def _bits(mask):
+    return [e for e in range(mask.bit_length()) if (mask >> e) & 1]
+
+
+def _mask(engs):
+    m = 0
+    for e in engs:
+        m |= 1 << e
+    return m
+
+
+def _common(topo, src, dsts):
+    m = topo.mask(src, dsts[0])
+    for d in dsts[1:]:
+        m &= topo.mask(src, d)
+    return m
+
+
+def _plan(T, topo):
+    cores = list(T.cores)
+    chips = []
+    for c in cores:
+        if topo.chip(c) not in chips:
+            chips.append(topo.chip(c))
+    mem = {ch: [c for c in cores if topo.chip(c) == ch] for ch in chips}
+    worker = {}
+    for ch in chips:
+        load = {}
+        far = {k: [mem[o][k] for o in chips if o != ch] for k in range(len(mem[ch]))}
+        for k, rc in enumerate(mem[ch]):
+            if all(topo.may_write(rc, d) for d in far[k]):
+                worker[ch, k] = rc
+                load[topo.die(rc)] = load.get(topo.die(rc), 0) + 1
+        spare = [c for c in range(NSIM) if topo.chip(c) == ch and c not in cores]
+        for k, rc in enumerate(mem[ch]):
+            if (ch, k) in worker:
+                continue
+            ok = [c for c in spare if c not in worker.values() and all(topo.may_write(c, d) for d in far[k])]
+            ok.sort(key=lambda c: (load.get(topo.die(c), 0), c))
+            worker[ch, k] = ok[0]
+            load[topo.die(ok[0])] = load.get(topo.die(ok[0]), 0) + 1
+    return cores, chips, mem, worker
+
+
+def _hop1(T, topo, plan, src):
+    cores, chips, mem, worker = plan
+    S = T.tables["SIGN"]
+    ch = topo.chip(src)
+    want = {1: [], -1: []}
+    for k, rc in enumerate(mem[ch]):
+        w = worker[ch, k]
+        s = S[cores.index(rc)][cores.index(src)]
+        if w != src and w not in want[s]:
+            want[s].append(w)
+    both = want[1] + want[-1]
+    engs = _bits(_common(topo, src, both))
+    if want[1] and want[-1]:
+        return [(1, engs[0::2], want[1]), (-1, engs[1::2], want[-1])]
+    s = 1 if want[1] else -1
+    return [(s, engs, want[s])]
+
+
+def _hop2(T, topo, plan, w):
+    cores, chips, mem, worker = plan
+    ch = topo.chip(w)
+    ks = [k for k in range(len(mem[ch])) if worker[ch, k] == w]
+    far, near = [], []
+    for i, k in enumerate(ks):
+        dsts = [mem[o][k] for o in chips if o != ch]
+        dsts.sort(key=lambda d: (topo.same_plane(ch, topo.chip(d)), d))
+        out = _bits(_common(topo, w, dsts))
+        n = len(out) // len(ks)
+        far.append((k, out[i * n:(i + 1) * n], dsts))
+        if mem[ch][k] != w:
+            rest = [e for e in _bits(topo.mask(w, mem[ch][k])) if e not in out]
+            m = len(rest) // len(ks)
+            near.append((k, rest[i * m:(i + 1) * m], [mem[ch][k]]))
+    return far, near
+
+
+def rank_program(g, core, T, topo):
+    plan = _plan(T, topo)
+    cores, chips, mem, worker = plan
+    S = T.tables["SIGN"]
+    rank = T.rank_of(core)
+    ch = topo.chip(core)
+    if ch not in chips or (rank is None and core not in worker.values()):
+        return
+    sem = T.sem
+    v = g.vector
+    ci = chips.index(ch)
+    my_ks = [k for k in range(len(mem[ch])) if worker[ch, k] == core]
+    sent = 0
+
+    def dst(c):
+        rid, pid, _ = topo.addr(c)
+        return DstId(rid=rid, pnc=pid)
+
+    if rank is not None:
+        g.sync.dma_start(T.xs[:], T.x[:]).then_inc(sem.ld, 16)
+        need_neg = any(S[cores.index(rc)][rank] < 0 for rc in mem[ch])
+        if need_neg:
+            v.memset(T.zp[:], 0.0).then_inc(sem.vz, 1)
+            v.wait_ge(sem.vz, 1)
+            v.wait_ge(sem.ld, 16)
+            v.tensor_tensor(T.nx[:], T.zp[:], T.xs[:], AluOpType.subtract).then_inc(sem.neg, 1)
+        g.wait_ge(sem.ld, 16)
+        if need_neg:
+            g.wait_ge(sem.neg, 1)
+        kp = mem[ch].index(core)
+        trs = []
+        for s, engs, ws in _hop1(T, topo, plan, core):
+            land = T["Lp%d" % kp] if s > 0 else T["Lm%d" % kp]
+            trs.append(RemoteDMATransfer(dst_ids=[dst(w) for w in ws], dma_engine_mask=_mask(engs),
+                                         remote_sem=sem.xin, srcs=[(T.xs if s > 0 else T.nx)[:]],
+                                         dsts=[land[:] for _ in ws], alu_op=0))
+            sent += len(engs)
+        g.remote_dma_fused(trs, local_sem=sem.sent)
+
+    def parts(k):
+        out = []
+        for kp, sc in enumerate(mem[ch]):
+            s = S[cores.index(mem[ch][k])][cores.index(sc)]
+            if sc == core:
+                out.append((T.xs if s > 0 else T.nx)[:])
+            else:
+                out.append((T["Lp%d" % kp] if s > 0 else T["Lm%d" % kp])[:])
+        return out
+
+    xin = 0
+    if my_ks:
+        for sc in mem[ch]:
+            if sc != core:
+                xin += sum(len(engs) for s, engs, ws in _hop1(T, topo, plan, sc) if core in ws)
+        g.wait_ge(sem.xin, xin)
+        for group in _hop2(T, topo, plan, core):
+            if not group:
+                continue
+            trs = []
+            for k, engs, dsts in group:
+                trs.append(RemoteDMATransfer(dst_ids=[dst(d) for d in dsts], dma_engine_mask=_mask(engs),
+                                             remote_sem=sem["u%d" % ci], srcs=parts(k),
+                                             dsts=[T["U%d" % ci][:] for _ in dsts], alu_op=1))
+                sent += len(engs)
+            g.remote_dma_fused(trs, local_sem=sem.sent)
+
+    if rank is not None:
+        k = mem[ch].index(core)
+        terms = []
+        if worker[ch, k] == core:
+            for i, ap in enumerate(parts(k)):
+                terms.append((ap, 1, [(sem.xin, xin), (sem.ld, 16)] + ([(sem.neg, 1)] if need_neg else [])))
+        else:
+            far, near = _hop2(T, topo, plan, worker[ch, k])
+            n = [len(engs) for kk, engs, dsts in near if kk == k][0]
+            terms.append((T["U%d" % ci][:], 1, [(sem["u%d" % ci], n)]))
+        others = [o for o in chips if o != ch]
+        others.sort(key=lambda o: (not topo.same_plane(ch, o), o))
+        for o in others:
+            hs = [S[rank][cores.index(sc)] * S[cores.index(mem[o][k])][cores.index(sc)] for sc in mem[o]]
+            assert min(hs) == max(hs)
+            far, near = _hop2(T, topo, plan, worker[o, k])
+            n = [len(engs) for kk, engs, dsts in far if kk == k][0]
+            oi = chips.index(o)
+            terms.append((T["U%d" % oi][:], hs[0], [(sem["u%d" % oi], n)]))
+        prev = None
+        for i, (ap, s, waits) in enumerate(terms):
+            for sm, val in waits:
+                v.wait_ge(sm, val)
+            if i == 0:
+                prev = ap
+                continue
+            if i >= 2:
+                v.wait_ge(sem.vc, i - 1)
+            last = i == len(terms) - 1
+            out = T.ys[:] if last else (T.pa if i % 2 else T.pb)[:]
+            op = AluOpType.add if s > 0 else AluOpType.subtract
+            v.tensor_tensor(out, prev, ap, op).then_inc(sem.fin if last else sem.vc, 1)
+            prev = out
+        g.sync.wait_ge(sem.fin, 1)
+        g.sync.dma_start(T.y[:], T.ys[:]).then_inc(sem.st, 16)
+        g.sync.wait_ge(sem.st, 16)
+
+    g.wait_ge(sem.sent, sent)

@@ -81,14 +81,20 @@ def _hop1(T, topo, plan, src):
     return [(s, engs, want[s])]
 
 
+def _turns(topo, chips, ch):
+    i = chips.index(ch)
+    ts = list(range(1, len(chips)))
+    ts.sort(key=lambda t: (topo.same_plane(chips[0], chips[t]), t))
+    return [chips[i ^ t] for t in ts]
+
+
 def _hop2(T, topo, plan, w):
     cores, chips, mem, worker = plan
     ch = topo.chip(w)
     ks = [k for k in range(len(mem[ch])) if worker[ch, k] == w]
     far, near = [], []
     for i, k in enumerate(ks):
-        dsts = [mem[o][k] for o in chips if o != ch]
-        dsts.sort(key=lambda d: (topo.same_plane(ch, topo.chip(d)), d))
+        dsts = [mem[o][k] for o in _turns(topo, chips, ch)]
         out = _bits(_common(topo, w, dsts))
         n = len(out) // len(ks)
         far.append((k, out[i * n:(i + 1) * n], dsts))
@@ -175,9 +181,7 @@ def rank_program(g, core, T, topo):
             far, near = _hop2(T, topo, plan, worker[ch, k])
             n = [len(engs) for kk, engs, dsts in near if kk == k][0]
             terms.append((T["U%d" % ci][:], 1, [(sem["u%d" % ci], n)]))
-        others = [o for o in chips if o != ch]
-        others.sort(key=lambda o: (not topo.same_plane(ch, o), o))
-        for o in others:
+        for o in _turns(topo, chips, ch):
             hs = [S[rank][cores.index(sc)] * S[cores.index(mem[o][k])][cores.index(sc)] for sc in mem[o]]
             assert min(hs) == max(hs)
             far, near = _hop2(T, topo, plan, worker[o, k])

from concourse.bass import DstId, RemoteDMATransfer
from concourse.mybir import AluOpType

NSIM = 112
P, C = 128, 256

SCRATCH = {
    "xs": ("sbuf", [P, C], "bfloat16"),
    "nx": ("sbuf", [P, C], "bfloat16"),
    "ys": ("sbuf", [P, C], "bfloat16"),
    "zp": ("psum", [P, C], "float32"),
    "pa": ("psum", [P, C], "float32"),
    "pb": ("psum", [P, C], "float32"),
}
for _i in range(4):
    SCRATCH["Lp%d" % _i] = ("sbuf", [P, C], "bfloat16")
    SCRATCH["Lm%d" % _i] = ("sbuf", [P, C], "bfloat16")
    SCRATCH["U%d" % _i] = ("sbuf", [P, C], "bfloat16")
SEMAPHORES = ["ld", "vz", "neg", "xin", "sent", "vc", "fin", "st", "u0", "u1", "u2", "u3"]


def _bits(mask):
    return [e for e in range(mask.bit_length()) if (mask >> e) & 1]


def _mask(engs):
    m = 0
    for e in engs:
        m |= 1 << e
    return m


def _common(topo, src, dsts):
    m = topo.mask(src, dsts[0])
    for d in dsts[1:]:
        m &= topo.mask(src, d)
    return m


def _plan(T, topo):
    cores = list(T.cores)
    chips = []
    for c in cores:
        if topo.chip(c) not in chips:
            chips.append(topo.chip(c))
    mem = {ch: [c for c in cores if topo.chip(c) == ch] for ch in chips}
    worker = {}
    for ch in chips:
        load = {}
        far = {k: [mem[o][k] for o in chips if o != ch] for k in range(len(mem[ch]))}
        for k, rc in enumerate(mem[ch]):
            if all(topo.may_write(rc, d) for d in far[k]):
                worker[ch, k] = rc
                load[topo.die(rc)] = load.get(topo.die(rc), 0) + 1
        spare = [c for c in range(NSIM) if topo.chip(c) == ch and c not in cores]
        for k, rc in enumerate(mem[ch]):
            if (ch, k) in worker:
                continue
            ok = [c for c in spare if c not in worker.values() and all(topo.may_write(c, d) for d in far[k])]
            ok.sort(key=lambda c: (load.get(topo.die(c), 0), c))
            worker[ch, k] = ok[0]
            load[topo.die(ok[0])] = load.get(topo.die(ok[0]), 0) + 1
    return cores, chips, mem, worker


def _hop1(T, topo, plan, src):
    cores, chips, mem, worker = plan
    S = T.tables["SIGN"]
    ch = topo.chip(src)
    want = {1: [], -1: []}
    for k, rc in enumerate(mem[ch]):
        w = worker[ch, k]
        s = S[cores.index(rc)][cores.index(src)]
        if w != src and w not in want[s]:
            want[s].append(w)
    both = want[1] + want[-1]
    engs = _bits(_common(topo, src, both))
    if want[1] and want[-1]:
        return [(1, engs[0::2], want[1]), (-1, engs[1::2], want[-1])]
    s = 1 if want[1] else -1
    return [(s, engs, want[s])]


def _turns(topo, chips, ch):
    i = chips.index(ch)
    ts = list(range(1, len(chips)))
    ts.sort(key=lambda t: (topo.same_plane(chips[0], chips[t]), t))
    return [chips[i ^ t] for t in ts]


def _hop2(T, topo, plan, w):
    cores, chips, mem, worker = plan
    ch = topo.chip(w)
    ks = [k for k in range(len(mem[ch])) if worker[ch, k] == w]
    far, near = [], []
    for i, k in enumerate(ks):
        dsts = [mem[o][k] for o in _turns(topo, chips, ch)]
        out = _bits(_common(topo, w, dsts))
        n = len(out) // len(ks)
        far.append((k, out[i * n:(i + 1) * n], dsts))
        if mem[ch][k] != w:
            rest = [e for e in _bits(topo.mask(w, mem[ch][k])) if e not in out]
            m = len(rest) // len(ks)
            near.append((k, rest[i * m:(i + 1) * m], [mem[ch][k]]))
    return far, near


def rank_program(g, core, T, topo):
    plan = _plan(T, topo)
    cores, chips, mem, worker = plan
    S = T.tables["SIGN"]
    rank = T.rank_of(core)
    ch = topo.chip(core)
    if ch not in chips or (rank is None and core not in worker.values()):
        return
    sem = T.sem
    v = g.vector
    ci = chips.index(ch)
    my_ks = [k for k in range(len(mem[ch])) if worker[ch, k] == core]
    sent = 0

    def dst(c):
        rid, pid, _ = topo.addr(c)
        return DstId(rid=rid, pnc=pid)

    if rank is not None:
        g.sync.dma_start(T.xs[:], T.x[:]).then_inc(sem.ld, 16)
        need_neg = any(S[cores.index(rc)][rank] < 0 for rc in mem[ch])
        if need_neg:
            v.memset(T.zp[:], 0.0).then_inc(sem.vz, 1)
            v.wait_ge(sem.vz, 1)
            v.wait_ge(sem.ld, 16)
            v.tensor_tensor(T.nx[:], T.zp[:], T.xs[:], AluOpType.subtract).then_inc(sem.neg, 1)
        g.wait_ge(sem.ld, 16)
        if need_neg:
            g.wait_ge(sem.neg, 1)
        kp = mem[ch].index(core)
        trs = []
        for s, engs, ws in _hop1(T, topo, plan, core):
            land = T["Lp%d" % kp] if s > 0 else T["Lm%d" % kp]
            trs.append(RemoteDMATransfer(dst_ids=[dst(w) for w in ws], dma_engine_mask=_mask(engs),
                                         remote_sem=sem.xin, srcs=[(T.xs if s > 0 else T.nx)[:]],
                                         dsts=[land[:] for _ in ws], alu_op=0))
            sent += len(engs)
        g.remote_dma_fused(trs, local_sem=sem.sent)

    def parts(k):
        out = []
        for kp, sc in enumerate(mem[ch]):
            s = S[cores.index(mem[ch][k])][cores.index(sc)]
            if sc == core:
                out.append((T.xs if s > 0 else T.nx)[:])
            else:
                out.append((T["Lp%d" % kp] if s > 0 else T["Lm%d" % kp])[:])
        return out

    xin = 0
    if my_ks:
        for sc in mem[ch]:
            if sc != core:
                xin += sum(len(engs) for s, engs, ws in _hop1(T, topo, plan, sc) if core in ws)
        g.wait_ge(sem.xin, xin)
        for group in _hop2(T, topo, plan, core):
            if not group:
                continue
            trs = []
            for k, engs, dsts in group:
                trs.append(RemoteDMATransfer(dst_ids=[dst(d) for d in dsts], dma_engine_mask=_mask(engs),
                                             remote_sem=sem["u%d" % ci], srcs=parts(k),
                                             dsts=[T["U%d" % ci][:] for _ in dsts], alu_op=1))
                sent += len(engs)
            g.remote_dma_fused(trs, local_sem=sem.sent)

    if rank is not None:
        k = mem[ch].index(core)
        terms = []
        if worker[ch, k] == core:
            for i, ap in enumerate(parts(k)):
                terms.append((ap, 1, [(sem.xin, xin), (sem.ld, 16)] + ([(sem.neg, 1)] if need_neg else [])))
        else:
            far, near = _hop2(T, topo, plan, worker[ch, k])
            n = [len(engs) for kk, engs, dsts in near if kk == k][0]
            terms.append((T["U%d" % ci][:], 1, [(sem["u%d" % ci], n)]))
        for o in _turns(topo, chips, ch):
            hs = [S[rank][cores.index(sc)] * S[cores.index(mem[o][k])][cores.index(sc)] for sc in mem[o]]
            assert min(hs) == max(hs)
            far, near = _hop2(T, topo, plan, worker[o, k])
            n = [len(engs) for kk, engs, dsts in far if kk == k][0]
            oi = chips.index(o)
            terms.append((T["U%d" % oi][:], hs[0], [(sem["u%d" % oi], n)]))
        prev = None
        for i, (ap, s, waits) in enumerate(terms):
            for sm, val in waits:
                v.wait_ge(sm, val)
            if i == 0:
                prev = ap
                continue
            if i >= 2:
                v.wait_ge(sem.vc, i - 1)
            last = i == len(terms) - 1
            out = T.ys[:] if last else (T.pa if i % 2 else T.pb)[:]
            op = AluOpType.add if s > 0 else AluOpType.subtract
            v.tensor_tensor(out, prev, ap, op).then_inc(sem.fin if last else sem.vc, 1)
            prev = out
        g.sync.wait_ge(sem.fin, 1)
        g.sync.dma_start(T.y[:], T.ys[:]).then_inc(sem.st, 16)
        g.sync.wait_ge(sem.st, 16)

    g.wait_ge(sem.sent, sent)
